import numpy as np, ml_dtypes
CORES = [21,29,37,45,53,61,69,77,85]
N = 9
NB, B = 8, 128
def setup_inputs(rng):
    return {"x": rng.standard_normal((N, 128, NB * B), dtype=np.float32).astype(ml_dtypes.bfloat16), "wv": (rng.standard_normal((N, 128, 128), dtype=np.float32) / 16).astype(ml_dtypes.bfloat16), "wh": (rng.standard_normal((N, 128, 128), dtype=np.float32) / 16).astype(ml_dtypes.bfloat16)}
def setup_inputs_big(rng):
    d = setup_inputs(rng)
    for k in ("x",): d[k] = (d[k].astype(np.float32) * 1048576.0).astype(d[k].dtype)
    return d
def setup_inputs_small(rng):
    d = setup_inputs(rng)
    for k in ("x",): d[k] = (d[k].astype(np.float32) * (1 / 1048576.0)).astype(d[k].dtype)
    return d
def setup_inputs_apart(rng):
    d = setup_inputs(rng)
    f = (10.0 ** rng.permutation(np.linspace(-1.5, 1.5, N))).astype(np.float32).reshape(N, 1, 1)
    for k in ("x",): d[k] = (d[k].astype(np.float32) * f).astype(d[k].dtype)
    return d
def reference(x, wv, wh):
    X, WV, WH = x.astype(np.float64), wv.astype(np.float64), wh.astype(np.float64)
    h = np.zeros((N, NB, 128, B))
    for r in range(N):
        for c in range(NB):
            a = X[r][:, B * c:B * c + B].copy()
            if r: a += WV[r].T @ h[r - 1][c]
            if c: a += WH[r].T @ h[r][c - 1]
            h[r][c] = np.maximum(a, 0.0)
    return {"y": np.concatenate([h[:, c] for c in range(NB)], axis=2).astype(ml_dtypes.bfloat16)}

@@ -1,0 +1,258 @@
+from concourse.bass import DstId, RemoteDMATransfer
+from concourse.mybir import AluOpType
+
+N, NB, B = 9, 8, 128
+K = 4
+LA = 6
+PIECES = (1, 4, 8)
+NBANK = 8
+WC = 2 * B
+NP = len(PIECES)
+
+SCRATCH = {
+    "up": ("sbuf", [128, NB * B], "bfloat16"),
+    "idn": ("sbuf", [128, B], "bfloat16"),
+    "zer": ("sbuf", [128, B], "bfloat16"),
+    "z": ("sbuf", [128, B + 1], "bfloat16"),
+    "di": ("dram", [B + 1, 128], "bfloat16"),
+}
+for _s in range(K):
+    SCRATCH["in%d" % _s] = ("sbuf", [128, WC + NB * B], "bfloat16")
+    SCRATCH["h%d" % _s] = ("sbuf", [128, NB * B], "bfloat16")
+for _b in range(NBANK):
+    SCRATCH["ps%d" % _b] = ("psum", [128, 512], "float32")
+
+SEMAPHORES = ["fill", "id1", "id2", "snt", "sty", "stc"]
+SEMAPHORES += ["ld%d" % p for p in range(NP)]
+SEMAPHORES += ["a%d_%d" % (s, p) for s in range(K) for p in range(NP)]
+SEMAPHORES += ["u%d" % c for c in range(NB)]
+SEMAPHORES += ["m%d" % n for n in range(K * NB)]
+SEMAPHORES += ["v%d" % n for n in range(K * NB)]
+
+
+def _bits(mask):
+    return [e for e in range(32) if (mask >> e) & 1]
+
+
+def _pick(mask, start, n):
+    m = 0
+    for e in _bits(mask)[start:start + n]:
+        m |= 1 << e
+    return m
+
+
+def _count(mask):
+    return len(_bits(mask))
+
+
+def _piece_cols(r, p):
+    lo = WC + PIECES[p - 1] * B if p else (0 if r else B)
+    return lo, WC + PIECES[p] * B
+
+
+def _piece_of(c):
+    for p in range(NP):
+        if c < PIECES[p]:
+            return p
+
+
+def _consumers(r):
+    return [q for q in range(r + 1, min(N - 1, r + K - 1) + 1)]
+
+
+def _plan(T, topo):
+    cores = list(T.cores)
+    relay = {}
+    for r in range(N):
+        home = cores[r]
+        far = [q for q in _consumers(r) if not topo.may_write(home, cores[q])]
+        cand = [c for c in range(topo.CORES_PER_CHIP * topo.CHIPS)
+                if topo.chip(c) == topo.chip(home) and c not in cores
+                and all(topo.may_write(c, cores[q]) for q in far)]
+        cand.sort(key=lambda c: (topo.die(c) != topo.die(home), c))
+        for j, q in enumerate(far):
+            relay[(r, q)] = cand[j]
+    return relay
+
+
+def _waiter(queue, T):
+    seen = {}
+
+    def w(name, val):
+        if seen.get(name, 0) < val:
+            queue.wait_ge(T.sem[name], val)
+            seen[name] = val
+    return w
+
+
+def _relay_program(g, core, T, topo, r, q, n_in):
+    dst = T.cores[q]
+    rid, pid, _ = topo.addr(dst)
+    mask = topo.mask(core, dst)
+    sent = 0
+    for p in range(NP):
+        lo, hi = _piece_cols(r, p)
+        g.wait_ge(T.sem["a0_%d" % p], n_in)
+        g.remote_dma(T["in%d" % (q - r)][:, lo:hi], T.in0[:, lo:hi], T.sem["a%d_%d" % (q - r, p)], T.sem.snt,
+                     pid, rid, mask)
+        sent += _count(mask)
+    g.wait_ge(T.sem.snt, sent)
+
+
+def _home_program(g, core, T, topo, q, relay):
+    cores = list(T.cores)
+    a = max(0, q - K + 1)
+    nr = q - a + 1
+    nblk = nr * NB
+    wt, wv_, wg = _waiter(g.tensor, T), _waiter(g.vector, T), _waiter(g, T)
+    wsy, wsc = _waiter(g.sync, T), _waiter(g.scalar, T)
+
+    g.vector.memset(T.z[:, 0:1], 1.0).then_inc(T.sem.fill, 1)
+    g.vector.memset(T.z[:, 1:B + 1], 0.0).then_inc(T.sem.fill, 1)
+    g.vector.memset(T.zer[:, :], 0.0).then_inc(T.sem.fill, 1)
+    ldn = [0] * NP
+    if q:
+        g.sync.dma_start(out=T.in0[:, 0:B], in_=T.wv[:, :]).then_inc(T.sem.ld0, 16)
+        ldn[0] += 16
+    g.scalar.dma_start(out=T.in0[:, B:WC], in_=T.wh[:, :]).then_inc(T.sem.ld0, 16)
+    ldn[0] += 16
+    g.sync.dma_start(out=T.in0[:, WC:WC + PIECES[0] * B], in_=T.x[:, 0:PIECES[0] * B]).then_inc(T.sem.ld0, 16)
+    ldn[0] += 16
+    wsc("fill", 3)
+    g.scalar.dma_start(out=T.di[:, :], in_=T.z[:, :]).then_inc(T.sem.id1, 16)
+    for p in range(1, NP):
+        qu = g.scalar if p % 2 else g.sync
+        qu.dma_start(out=T.in0[:, WC + PIECES[p - 1] * B:WC + PIECES[p] * B],
+                     in_=T.x[:, PIECES[p - 1] * B:PIECES[p] * B]).then_inc(T.sem["ld%d" % p], 16)
+        ldn[p] += 16
+    wsc("id1", 16)
+    g.scalar.dma_start(out=T.idn[:, :], in_=T.di[0:B, :]).then_inc(T.sem.id2, 16)
+
+    sent = 0
+    far = [c for c in _consumers(q) if (q, c) in relay]
+    near = [c for c in _consumers(q) if (q, c) not in relay]
+    for p in range(NP):
+        lo, hi = _piece_cols(q, p)
+        if far or near:
+            wg("ld%d" % p, ldn[p])
+        if far:
+            trs = []
+            for j, c in enumerate(far):
+                hc = relay[(q, c)]
+                rid, pid, _ = topo.addr(hc)
+                full = topo.mask(core, hc)
+                ne = _count(full) // (2 if len(far) > 1 else 1)
+                m = _pick(full, j * ne, ne)
+                trs.append(RemoteDMATransfer(dst_ids=[DstId(rid=rid, pnc=pid)], dma_engine_mask=m,
+                                             remote_sem=T.sem["a0_%d" % p], src=T.in0[:, lo:hi], dst=T.in0[:, lo:hi]))
+                sent += ne
+            g.remote_dma_fused(trs, local_sem=T.sem.snt)
+        for c in near:
+            rid, pid, _ = topo.addr(cores[c])
+            m = topo.mask(core, cores[c])
+            g.remote_dma(T["in%d" % (c - q)][:, lo:hi], T.in0[:, lo:hi], T.sem["a%d_%d" % (c - q, p)], T.sem.snt,
+                         pid, rid, m)
+            sent += _count(m)
+
+    def in_dep(i, p):
+        r = a + i
+        if r == q:
+            return "ld%d" % p, ldn[p]
+        src = relay.get((r, q), cores[r])
+        return "a%d_%d" % (q - r, p), _count(topo.mask(src, core))
+
+    up_n = _count(topo.mask(cores[q - K], core)) if a else 0
+
+    def has_h(n):
+        return n // nr > 0
+
+    def has_v(n):
+        return n % nr > 0 or a > 0
+
+    ops = [("x", m) for m in range(min(LA, nblk))]
+    for n in range(nblk):
+        if has_v(n):
+            ops.append(("v", n))
+        m = n + nr - 1
+        if m < nblk and has_h(m):
+            ops.append(("h", m))
+        if n + LA < nblk:
+            ops.append(("x", n + LA))
+    last = {}
+    for k, (_, n) in enumerate(ops):
+        last[n] = k
+
+    for k, (kind, n) in enumerate(ops):
+        c, i = divmod(n, nr)
+        s = q - (a + i)
+        inb = T["in%d" % s]
+        out = T["ps%d" % (n % NBANK)][:, 0:B]
+        cs = slice(c * B, (c + 1) * B)
+        if kind == "x":
+            wt(*in_dep(i, _piece_of(c)))
+            wt("id2", 16)
+            if n >= NBANK:
+                wt("v%d" % (n - NBANK), 1)
+            ins = g.tensor.matmul(out, T.idn[:, :], inb[:, WC + c * B:WC + (c + 1) * B], True, last[n] == k)
+        elif kind == "h":
+            wt(*in_dep(i, 0))
+            wt("v%d" % (n - nr), 1)
+            ins = g.tensor.matmul(out, inb[:, B:WC], T["h%d" % s][:, (c - 1) * B:c * B], False, last[n] == k)
+        else:
+            wt(*in_dep(i, 0))
+            if i:
+                wt("v%d" % (n - 1), 1)
+                rhs = T["h%d" % (s + 1)][:, cs]
+            else:
+                wt("u%d" % c, up_n)
+                rhs = T.up[:, cs]
+            ins = g.tensor.matmul(out, inb[:, 0:B], rhs, False, last[n] == k)
+        if last[n] == k:
+            ins.then_inc(T.sem["m%d" % n], 1)
+
+    wv_("fill", 3)
+    for n in range(nblk):
+        c, i = divmod(n, nr)
+        s = q - (a + i)
+        wv_("m%d" % n, 1)
+        g.vector.tensor_tensor(T["h%d" % s][:, c * B:(c + 1) * B], T["ps%d" % (n % NBANK)][:, 0:B], T.zer[:, :],
+                               AluOpType.max).then_inc(T.sem["v%d" % n], 1)
+
+    if q + K < N:
+        dst = cores[q + K]
+        rid, pid, _ = topo.addr(dst)
+        m = topo.mask(core, dst)
+        for c in range(NB):
+            wg("v%d" % (c * nr + nr - 1), 1)
+            g.remote_dma(T.up[:, c * B:(c + 1) * B], T.h0[:, c * B:(c + 1) * B], T.sem["u%d" % c], T.sem.snt,
+                         pid, rid, m)
+            sent += _count(m)
+        groups = [(0, 4), (4, 8)]
+    else:
+        groups = [(0, 4), (4, 6), (6, 7), (7, 8)]
+    if sent:
+        g.wait_ge(T.sem.snt, sent)
+
+    tot = {"sty": 0, "stc": 0}
+    for k, (c0, c1) in enumerate(groups):
+        qu, w, name = ((g.sync, wsy, "sty"), (g.scalar, wsc, "stc"))[k % 2]
+        for c in range(c0, c1):
+            w("v%d" % (c * nr + nr - 1), 1)
+        qu.dma_start(out=T.y[:, c0 * B:c1 * B], in_=T.h0[:, c0 * B:c1 * B]).then_inc(T.sem[name], 16)
+        tot[name] += 16
+    wsy("sty", tot["sty"])
+    wsc("stc", tot["stc"])
+
+
+def rank_program(g, core, T, topo):
+    relay = _plan(T, topo)
+    q = T.rank_of(core)
+    if q is not None:
+        _home_program(g, core, T, topo, q, relay)
+        return
+    for (r, c), hc in relay.items():
+        if hc == core:
+            nfar = len([1 for (r2, _c) in relay if r2 == r])
+            n_in = _count(topo.mask(T.cores[r], core)) // (2 if nfar > 1 else 1)
+            _relay_program(g, core, T, topo, r, c, n_in)
+            return

@@ -3,11 +3,12 @@ from concourse.mybir import AluOpType
 
 N, NB, B = 9, 8, 128
 K = 4
-LA = 6
 PIECES = (1, 4, 8)
 NBANK = 8
-WC = 2 * B
 NP = len(PIECES)
+NH = 2
+W = B // NH
+LX = NBANK // NH - 1
 
 SCRATCH = {
     "up": ("sbuf", [128, NB * B], "bfloat16"),
@@ -17,7 +18,7 @@ SCRATCH = {
     "di": ("dram", [B + 1, 128], "bfloat16"),
 }
 for _s in range(K):
-    SCRATCH["in%d" % _s] = ("sbuf", [128, WC + NB * B], "bfloat16")
+    SCRATCH["in%d" % _s] = ("sbuf", [128, (NB + 2) * B], "bfloat16")
     SCRATCH["h%d" % _s] = ("sbuf", [128, NB * B], "bfloat16")
 for _b in range(NBANK):
     SCRATCH["ps%d" % _b] = ("psum", [128, 512], "float32")
@@ -26,8 +27,8 @@ SEMAPHORES = ["fill", "id1", "id2", "snt", "sty", "stc"]
 SEMAPHORES += ["ld%d" % p for p in range(NP)]
 SEMAPHORES += ["a%d_%d" % (s, p) for s in range(K) for p in range(NP)]
 SEMAPHORES += ["u%d" % c for c in range(NB)]
-SEMAPHORES += ["m%d" % n for n in range(K * NB)]
-SEMAPHORES += ["v%d" % n for n in range(K * NB)]
+SEMAPHORES += ["m%d" % b for b in range(NBANK)]
+SEMAPHORES += ["v%d_%d" % (n, j) for n in range(K * NB) for j in range(NH)]
 
 
 def _bits(mask):
@@ -45,9 +46,17 @@ def _count(mask):
     return len(_bits(mask))
 
 
+def _xcol(c):
+    return B if c == 0 else (c + 2) * B
+
+
+def _piece_end(p):
+    return 2 * B if p == 0 else (2 + PIECES[p]) * B
+
+
 def _piece_cols(r, p):
-    lo = WC + PIECES[p - 1] * B if p else (0 if r else B)
-    return lo, WC + PIECES[p] * B
+    lo = _piece_end(p - 1) if p else (0 if r else B)
+    return lo, _piece_end(p)
 
 
 def _piece_of(c):
@@ -69,7 +78,7 @@ def _plan(T, topo):
         cand = [c for c in range(topo.CORES_PER_CHIP * topo.CHIPS)
                 if topo.chip(c) == topo.chip(home) and c not in cores
                 and all(topo.may_write(c, cores[q]) for q in far)]
-        cand.sort(key=lambda c: (topo.die(c) != topo.die(home), c))
+        cand.sort(key=lambda c: (topo.die(c) == topo.die(home), c))
         for j, q in enumerate(far):
             relay[(r, q)] = cand[j]
     return relay
@@ -114,45 +123,73 @@ def _home_program(g, core, T, topo, q, relay):
     if q:
         g.sync.dma_start(out=T.in0[:, 0:B], in_=T.wv[:, :]).then_inc(T.sem.ld0, 16)
         ldn[0] += 16
-    g.scalar.dma_start(out=T.in0[:, B:WC], in_=T.wh[:, :]).then_inc(T.sem.ld0, 16)
+    g.scalar.dma_start(out=T.in0[:, B:2 * B], in_=T.x[:, 0:B]).then_inc(T.sem.ld0, 16)
     ldn[0] += 16
-    g.sync.dma_start(out=T.in0[:, WC:WC + PIECES[0] * B], in_=T.x[:, 0:PIECES[0] * B]).then_inc(T.sem.ld0, 16)
-    ldn[0] += 16
+    g.sync.dma_start(out=T.in0[:, 2 * B:3 * B], in_=T.wh[:, :]).then_inc(T.sem.ld1, 16)
+    ldn[1] += 16
     wsc("fill", 3)
     g.scalar.dma_start(out=T.di[:, :], in_=T.z[:, :]).then_inc(T.sem.id1, 16)
     for p in range(1, NP):
         qu = g.scalar if p % 2 else g.sync
-        qu.dma_start(out=T.in0[:, WC + PIECES[p - 1] * B:WC + PIECES[p] * B],
+        qu.dma_start(out=T.in0[:, (2 + PIECES[p - 1]) * B:(2 + PIECES[p]) * B],
                      in_=T.x[:, PIECES[p - 1] * B:PIECES[p] * B]).then_inc(T.sem["ld%d" % p], 16)
         ldn[p] += 16
     wsc("id1", 16)
     g.scalar.dma_start(out=T.idn[:, :], in_=T.di[0:B, :]).then_inc(T.sem.id2, 16)
 
-    sent = 0
+    sent = [0]
     far = [c for c in _consumers(q) if (q, c) in relay]
     near = [c for c in _consumers(q) if (q, c) not in relay]
-    for p in range(NP):
+
+    def send_far(p):
+        if not far:
+            return
         lo, hi = _piece_cols(q, p)
-        if far or near:
-            wg("ld%d" % p, ldn[p])
-        if far:
-            trs = []
-            for j, c in enumerate(far):
-                hc = relay[(q, c)]
-                rid, pid, _ = topo.addr(hc)
-                full = topo.mask(core, hc)
-                ne = _count(full) // (2 if len(far) > 1 else 1)
-                m = _pick(full, j * ne, ne)
-                trs.append(RemoteDMATransfer(dst_ids=[DstId(rid=rid, pnc=pid)], dma_engine_mask=m,
-                                             remote_sem=T.sem["a0_%d" % p], src=T.in0[:, lo:hi], dst=T.in0[:, lo:hi]))
-                sent += ne
-            g.remote_dma_fused(trs, local_sem=T.sem.snt)
+        wg("ld%d" % p, ldn[p])
+        trs = []
+        for j, c in enumerate(far):
+            hc = relay[(q, c)]
+            rid, pid, _ = topo.addr(hc)
+            full = topo.mask(core, hc)
+            ne = _count(full) // (2 if len(far) > 1 else 1)
+            trs.append(RemoteDMATransfer(dst_ids=[DstId(rid=rid, pnc=pid)], dma_engine_mask=_pick(full, j * ne, ne),
+                                         remote_sem=T.sem["a0_%d" % p], src=T.in0[:, lo:hi], dst=T.in0[:, lo:hi]))
+            sent[0] += ne
+        g.remote_dma_fused(trs, local_sem=T.sem.snt)
+
+    def send_near(p):
+        lo, hi = _piece_cols(q, p)
         for c in near:
+            wg("ld%d" % p, ldn[p])
             rid, pid, _ = topo.addr(cores[c])
             m = topo.mask(core, cores[c])
             g.remote_dma(T["in%d" % (c - q)][:, lo:hi], T.in0[:, lo:hi], T.sem["a%d_%d" % (c - q, p)], T.sem.snt,
                          pid, rid, m)
-            sent += _count(m)
+            sent[0] += _count(m)
+
+    def send_h(c):
+        dst = cores[q + K]
+        rid, pid, _ = topo.addr(dst)
+        m = topo.mask(core, dst)
+        for j in range(NH):
+            wg("v%d_%d" % (c * nr + nr - 1, j), 1)
+        g.remote_dma(T.up[:, c * B:(c + 1) * B], T.h0[:, c * B:(c + 1) * B], T.sem["u%d" % c], T.sem.snt,
+                     pid, rid, m)
+        sent[0] += _count(m)
+
+    hleft = list(range(NB)) if q + K < N else []
+    early = nr == 1
+    send_far(0)
+    for p in range(1, NP):
+        send_far(p)
+        send_near(p - 1)
+        if early and hleft:
+            send_h(hleft.pop(0))
+    send_near(NP - 1)
+    for c in hleft:
+        send_h(c)
+    if sent[0]:
+        g.wait_ge(T.sem.snt, sent[0])
 
     def in_dep(i, p):
         r = a + i
@@ -169,15 +206,16 @@ def _home_program(g, core, T, topo, q, relay):
     def has_v(n):
         return n % nr > 0 or a > 0
 
-    ops = [("x", m) for m in range(min(LA, nblk))]
+    lh = min(LX - 1, nr - 1)
+    ops = [("x", m) for m in range(min(LX, nblk))]
+    ops += [("h", m) for m in range(min(lh, nblk)) if has_h(m)]
     for n in range(nblk):
         if has_v(n):
             ops.append(("v", n))
-        m = n + nr - 1
-        if m < nblk and has_h(m):
-            ops.append(("h", m))
-        if n + LA < nblk:
-            ops.append(("x", n + LA))
+        if n + lh < nblk and has_h(n + lh):
+            ops.append(("h", n + lh))
+        if n + LX < nblk:
+            ops.append(("x", n + LX))
     last = {}
     for k, (_, n) in enumerate(ops):
         last[n] = k
@@ -186,58 +224,51 @@ def _home_program(g, core, T, topo, q, relay):
         c, i = divmod(n, nr)
         s = q - (a + i)
         inb = T["in%d" % s]
-        out = T["ps%d" % (n % NBANK)][:, 0:B]
-        cs = slice(c * B, (c + 1) * B)
-        if kind == "x":
-            wt(*in_dep(i, _piece_of(c)))
-            wt("id2", 16)
-            if n >= NBANK:
-                wt("v%d" % (n - NBANK), 1)
-            ins = g.tensor.matmul(out, T.idn[:, :], inb[:, WC + c * B:WC + (c + 1) * B], True, last[n] == k)
-        elif kind == "h":
-            wt(*in_dep(i, 0))
-            wt("v%d" % (n - nr), 1)
-            ins = g.tensor.matmul(out, inb[:, B:WC], T["h%d" % s][:, (c - 1) * B:c * B], False, last[n] == k)
-        else:
-            wt(*in_dep(i, 0))
-            if i:
-                wt("v%d" % (n - 1), 1)
-                rhs = T["h%d" % (s + 1)][:, cs]
+        for j in range(NH):
+            bank = (n * NH + j) % NBANK
+            out = T["ps%d" % bank][:, 0:W]
+            o = j * W
+            if kind == "x":
+                wt(*in_dep(i, _piece_of(c)))
+                wt("id2", 16)
+                if n * NH >= NBANK:
+                    wt("v%d_%d" % (n - NBANK // NH, j), 1)
+                ins = g.tensor.matmul(out, T.idn[:, :], inb[:, _xcol(c) + o:_xcol(c) + o + W], True, last[n] == k)
+            elif kind == "h":
+                wt(*in_dep(i, 1))
+                wt("v%d_%d" % (n - nr, j), 1)
+                ins = g.tensor.matmul(out, inb[:, 2 * B:3 * B], T["h%d" % s][:, (c - 1) * B + o:(c - 1) * B + o + W],
+                                      False, last[n] == k)
             else:
-                wt("u%d" % c, up_n)
-                rhs = T.up[:, cs]
-            ins = g.tensor.matmul(out, inb[:, 0:B], rhs, False, last[n] == k)
-        if last[n] == k:
-            ins.then_inc(T.sem["m%d" % n], 1)
+                wt(*in_dep(i, 0))
+                if i:
+                    wt("v%d_%d" % (n - 1, j), 1)
+                    rhs = T["h%d" % (s + 1)][:, c * B + o:c * B + o + W]
+                else:
+                    wt("u%d" % c, up_n)
+                    rhs = T.up[:, c * B + o:c * B + o + W]
+                ins = g.tensor.matmul(out, inb[:, 0:B], rhs, False, last[n] == k)
+            if last[n] == k:
+                ins.then_inc(T.sem["m%d" % bank], 1)
 
     wv_("fill", 3)
     for n in range(nblk):
         c, i = divmod(n, nr)
         s = q - (a + i)
-        wv_("m%d" % n, 1)
-        g.vector.tensor_tensor(T["h%d" % s][:, c * B:(c + 1) * B], T["ps%d" % (n % NBANK)][:, 0:B], T.zer[:, :],
-                               AluOpType.max).then_inc(T.sem["v%d" % n], 1)
+        for j in range(NH):
+            u = n * NH + j
+            wv_("m%d" % (u % NBANK), u // NBANK + 1)
+            g.vector.tensor_tensor(T["h%d" % s][:, c * B + j * W:c * B + (j + 1) * W],
+                                   T["ps%d" % (u % NBANK)][:, 0:W], T.zer[:, 0:W],
+                                   AluOpType.max).then_inc(T.sem["v%d_%d" % (n, j)], 1)
 
-    if q + K < N:
-        dst = cores[q + K]
-        rid, pid, _ = topo.addr(dst)
-        m = topo.mask(core, dst)
-        for c in range(NB):
-            wg("v%d" % (c * nr + nr - 1), 1)
-            g.remote_dma(T.up[:, c * B:(c + 1) * B], T.h0[:, c * B:(c + 1) * B], T.sem["u%d" % c], T.sem.snt,
-                         pid, rid, m)
-            sent += _count(m)
-        groups = [(0, 4), (4, 8)]
-    else:
-        groups = [(0, 4), (4, 6), (6, 7), (7, 8)]
-    if sent:
-        g.wait_ge(T.sem.snt, sent)
-
+    groups = [(0, 4), (4, 8)] if q + K < N else [(0, 4), (4, 6), (6, 7), (7, 8)]
     tot = {"sty": 0, "stc": 0}
     for k, (c0, c1) in enumerate(groups):
         qu, w, name = ((g.sync, wsy, "sty"), (g.scalar, wsc, "stc"))[k % 2]
         for c in range(c0, c1):
-            w("v%d" % (c * nr + nr - 1), 1)
+            for j in range(NH):
+                w("v%d_%d" % (c * nr + nr - 1, j), 1)
         qu.dma_start(out=T.y[:, c0 * B:c1 * B], in_=T.h0[:, c0 * B:c1 * B]).then_inc(T.sem[name], 16)
         tot[name] += 16
     wsy("sty", tot["sty"])

@@ -8,7 +8,7 @@ NBANK = 8
 NP = len(PIECES)
 NH = 2
 W = B // NH
-LX = NBANK // NH - 1
+INFL = NBANK // NH
 
 SCRATCH = {
     "up": ("sbuf", [128, NB * B], "bfloat16"),
@@ -69,6 +69,12 @@ def _consumers(r):
     return [q for q in range(r + 1, min(N - 1, r + K - 1) + 1)]
 
 
+def _hgroups(r):
+    if r == 0:
+        return [((PIECES[p - 1] if p else 0), PIECES[p]) for p in range(NP)]
+    return [(c, c + 1) for c in range(NB)]
+
+
 def _plan(T, topo):
     cores = list(T.cores)
     relay = {}
@@ -84,6 +90,28 @@ def _plan(T, topo):
     return relay
 
 
+def _far_masks(T, topo, relay, r, p):
+    cores = list(T.cores)
+    home = cores[r]
+    far = [q for q in _consumers(r) if (r, q) in relay]
+    near = [q for q in _consumers(r) if (r, q) not in relay]
+    if not far:
+        return {}
+    full = topo.mask(home, relay[(r, far[0])])
+    leave = full & topo.mask(home, cores[far[0]])
+    stay = full & ~leave
+    streams_off = len(near) + (1 if r == 0 and r + K < N else 0)
+    wide = NP if streams_off == 0 else (2 if streams_off == 1 else 1)
+    if p < wide:
+        if len(far) == 1:
+            return {far[0]: full}
+        return {far[0]: leave, far[1]: stay}
+    if len(far) == 1:
+        return {far[0]: stay}
+    half = _count(stay) // 2
+    return {far[0]: _pick(stay, 0, half), far[1]: _pick(stay, half, half)}
+
+
 def _waiter(queue, T):
     seen = {}
 
@@ -94,14 +122,14 @@ def _waiter(queue, T):
     return w
 
 
-def _relay_program(g, core, T, topo, r, q, n_in):
+def _relay_program(g, core, T, topo, relay, r, q):
     dst = T.cores[q]
     rid, pid, _ = topo.addr(dst)
     mask = topo.mask(core, dst)
     sent = 0
     for p in range(NP):
         lo, hi = _piece_cols(r, p)
-        g.wait_ge(T.sem["a0_%d" % p], n_in)
+        g.wait_ge(T.sem["a0_%d" % p], _count(_far_masks(T, topo, relay, r, p)[q]))
         g.remote_dma(T["in%d" % (q - r)][:, lo:hi], T.in0[:, lo:hi], T.sem["a%d_%d" % (q - r, p)], T.sem.snt,
                      pid, rid, mask)
         sent += _count(mask)
@@ -112,9 +140,11 @@ def _home_program(g, core, T, topo, q, relay):
     cores = list(T.cores)
     a = max(0, q - K + 1)
     nr = q - a + 1
-    nblk = nr * NB
     wt, wv_, wg = _waiter(g.tensor, T), _waiter(g.vector, T), _waiter(g, T)
     wsy, wsc = _waiter(g.sync, T), _waiter(g.scalar, T)
+
+    def vname(i, c, j):
+        return "v%d_%d" % (c * nr + i, j)
 
     g.vector.memset(T.z[:, 0:1], 1.0).then_inc(T.sem.fill, 1)
     g.vector.memset(T.z[:, 1:B + 1], 0.0).then_inc(T.sem.fill, 1)
@@ -138,23 +168,20 @@ def _home_program(g, core, T, topo, q, relay):
     g.scalar.dma_start(out=T.idn[:, :], in_=T.di[0:B, :]).then_inc(T.sem.id2, 16)
 
     sent = [0]
-    far = [c for c in _consumers(q) if (q, c) in relay]
     near = [c for c in _consumers(q) if (q, c) not in relay]
 
     def send_far(p):
-        if not far:
+        masks = _far_masks(T, topo, relay, q, p)
+        if not masks:
             return
         lo, hi = _piece_cols(q, p)
         wg("ld%d" % p, ldn[p])
         trs = []
-        for j, c in enumerate(far):
-            hc = relay[(q, c)]
-            rid, pid, _ = topo.addr(hc)
-            full = topo.mask(core, hc)
-            ne = _count(full) // (2 if len(far) > 1 else 1)
-            trs.append(RemoteDMATransfer(dst_ids=[DstId(rid=rid, pnc=pid)], dma_engine_mask=_pick(full, j * ne, ne),
+        for c, m in masks.items():
+            rid, pid, _ = topo.addr(relay[(q, c)])
+            trs.append(RemoteDMATransfer(dst_ids=[DstId(rid=rid, pnc=pid)], dma_engine_mask=m,
                                          remote_sem=T.sem["a0_%d" % p], src=T.in0[:, lo:hi], dst=T.in0[:, lo:hi]))
-            sent[0] += ne
+            sent[0] += _count(m)
         g.remote_dma_fused(trs, local_sem=T.sem.snt)
 
     def send_near(p):
@@ -167,27 +194,28 @@ def _home_program(g, core, T, topo, q, relay):
                          pid, rid, m)
             sent[0] += _count(m)
 
-    def send_h(c):
+    def send_h(k):
+        c0, c1 = _hgroups(q)[k]
         dst = cores[q + K]
         rid, pid, _ = topo.addr(dst)
         m = topo.mask(core, dst)
-        for j in range(NH):
-            wg("v%d_%d" % (c * nr + nr - 1, j), 1)
-        g.remote_dma(T.up[:, c * B:(c + 1) * B], T.h0[:, c * B:(c + 1) * B], T.sem["u%d" % c], T.sem.snt,
-                     pid, rid, m)
+        for c in range(c0, c1):
+            for j in range(NH):
+                wg(vname(nr - 1, c, j), 1)
+        g.remote_dma(T.up[:, c0 * B:c1 * B], T.h0[:, c0 * B:c1 * B], T.sem["u%d" % k], T.sem.snt, pid, rid, m)
         sent[0] += _count(m)
 
-    hleft = list(range(NB)) if q + K < N else []
-    early = nr == 1
+    hleft = list(range(len(_hgroups(q)))) if q + K < N else []
+    early = q == 0
     send_far(0)
     for p in range(1, NP):
         send_far(p)
         send_near(p - 1)
-        if early and hleft:
+        if early and hleft and p > 1:
             send_h(hleft.pop(0))
     send_near(NP - 1)
-    for c in hleft:
-        send_h(c)
+    for k in hleft:
+        send_h(k)
     if sent[0]:
         g.wait_ge(T.sem.snt, sent[0])
 
@@ -199,68 +227,69 @@ def _home_program(g, core, T, topo, q, relay):
         return "a%d_%d" % (q - r, p), _count(topo.mask(src, core))
 
     up_n = _count(topo.mask(cores[q - K], core)) if a else 0
+    up_k = {}
+    if a:
+        for k, (c0, c1) in enumerate(_hgroups(q - K)):
+            for c in range(c0, c1):
+                up_k[c] = k
 
-    def has_h(n):
-        return n // nr > 0
-
-    def has_v(n):
-        return n % nr > 0 or a > 0
-
-    lh = min(LX - 1, nr - 1)
-    ops = [("x", m) for m in range(min(LX, nblk))]
-    ops += [("h", m) for m in range(min(lh, nblk)) if has_h(m)]
-    for n in range(nblk):
-        if has_v(n):
-            ops.append(("v", n))
-        if n + lh < nblk and has_h(n + lh):
-            ops.append(("h", n + lh))
-        if n + LX < nblk:
-            ops.append(("x", n + LX))
+    order = []
+    for d in range(nr + NB - 1):
+        for i in range(min(nr - 1, d), max(0, d - NB + 1) - 1, -1):
+            order.append((i, d - i))
+    ops = [("x", 0)]
+    for t, (i, c) in enumerate(order):
+        if c > 0:
+            ops.append(("h", t))
+        if i > 0 or a > 0:
+            ops.append(("v", t))
+        if t + 1 < len(order):
+            ops.append(("x", t + 1))
     last = {}
-    for k, (_, n) in enumerate(ops):
-        last[n] = k
+    for k, (_, t) in enumerate(ops):
+        last[t] = k
 
-    for k, (kind, n) in enumerate(ops):
-        c, i = divmod(n, nr)
+    for k, (kind, t) in enumerate(ops):
+        i, c = order[t]
         s = q - (a + i)
         inb = T["in%d" % s]
         for j in range(NH):
-            bank = (n * NH + j) % NBANK
+            bank = (t * NH + j) % NBANK
             out = T["ps%d" % bank][:, 0:W]
             o = j * W
             if kind == "x":
                 wt(*in_dep(i, _piece_of(c)))
                 wt("id2", 16)
-                if n * NH >= NBANK:
-                    wt("v%d_%d" % (n - NBANK // NH, j), 1)
-                ins = g.tensor.matmul(out, T.idn[:, :], inb[:, _xcol(c) + o:_xcol(c) + o + W], True, last[n] == k)
+                if t >= INFL:
+                    i0, c0 = order[t - INFL]
+                    wt(vname(i0, c0, j), 1)
+                ins = g.tensor.matmul(out, T.idn[:, :], inb[:, _xcol(c) + o:_xcol(c) + o + W], True, last[t] == k)
             elif kind == "h":
                 wt(*in_dep(i, 1))
-                wt("v%d_%d" % (n - nr, j), 1)
+                wt(vname(i, c - 1, j), 1)
                 ins = g.tensor.matmul(out, inb[:, 2 * B:3 * B], T["h%d" % s][:, (c - 1) * B + o:(c - 1) * B + o + W],
-                                      False, last[n] == k)
+                                      False, last[t] == k)
             else:
                 wt(*in_dep(i, 0))
                 if i:
-                    wt("v%d_%d" % (n - 1, j), 1)
+                    wt(vname(i - 1, c, j), 1)
                     rhs = T["h%d" % (s + 1)][:, c * B + o:c * B + o + W]
                 else:
-                    wt("u%d" % c, up_n)
+                    wt("u%d" % up_k[c], up_n)
                     rhs = T.up[:, c * B + o:c * B + o + W]
-                ins = g.tensor.matmul(out, inb[:, 0:B], rhs, False, last[n] == k)
-            if last[n] == k:
+                ins = g.tensor.matmul(out, inb[:, 0:B], rhs, False, last[t] == k)
+            if last[t] == k:
                 ins.then_inc(T.sem["m%d" % bank], 1)
 
     wv_("fill", 3)
-    for n in range(nblk):
-        c, i = divmod(n, nr)
+    for t, (i, c) in enumerate(order):
         s = q - (a + i)
         for j in range(NH):
-            u = n * NH + j
+            u = t * NH + j
             wv_("m%d" % (u % NBANK), u // NBANK + 1)
             g.vector.tensor_tensor(T["h%d" % s][:, c * B + j * W:c * B + (j + 1) * W],
                                    T["ps%d" % (u % NBANK)][:, 0:W], T.zer[:, 0:W],
-                                   AluOpType.max).then_inc(T.sem["v%d_%d" % (n, j)], 1)
+                                   AluOpType.max).then_inc(T.sem[vname(i, c, j)], 1)
 
     groups = [(0, 4), (4, 8)] if q + K < N else [(0, 4), (4, 6), (6, 7), (7, 8)]
     tot = {"sty": 0, "stc": 0}
@@ -268,7 +297,7 @@ def _home_program(g, core, T, topo, q, relay):
         qu, w, name = ((g.sync, wsy, "sty"), (g.scalar, wsc, "stc"))[k % 2]
         for c in range(c0, c1):
             for j in range(NH):
-                w("v%d_%d" % (c * nr + nr - 1, j), 1)
+                w(vname(nr - 1, c, j), 1)
         qu.dma_start(out=T.y[:, c0 * B:c1 * B], in_=T.h0[:, c0 * B:c1 * B]).then_inc(T.sem[name], 16)
         tot[name] += 16
     wsy("sty", tot["sty"])
@@ -283,7 +312,5 @@ def rank_program(g, core, T, topo):
         return
     for (r, c), hc in relay.items():
         if hc == core:
-            nfar = len([1 for (r2, _c) in relay if r2 == r])
-            n_in = _count(topo.mask(T.cores[r], core)) // (2 if nfar > 1 else 1)
-            _relay_program(g, core, T, topo, r, c, n_in)
+            _relay_program(g, core, T, topo, relay, r, c)
             return

@@ -14,8 +14,7 @@ SCRATCH = {
     "up": ("sbuf", [128, NB * B], "bfloat16"),
     "idn": ("sbuf", [128, B], "bfloat16"),
     "zer": ("sbuf", [128, B], "bfloat16"),
-    "z": ("sbuf", [128, B + 1], "bfloat16"),
-    "di": ("dram", [B + 1, 128], "bfloat16"),
+    "one": ("sbuf", [128, B], "bfloat16"),
 }
 for _s in range(K):
     SCRATCH["in%d" % _s] = ("sbuf", [128, (NB + 2) * B], "bfloat16")
@@ -23,7 +22,7 @@ for _s in range(K):
 for _b in range(NBANK):
     SCRATCH["ps%d" % _b] = ("psum", [128, 512], "float32")
 
-SEMAPHORES = ["fill", "id1", "id2", "snt", "sty", "stc"]
+SEMAPHORES = ["fill", "fone", "idg", "id2", "snt", "sty", "stc"]
 SEMAPHORES += ["ld%d" % p for p in range(NP)]
 SEMAPHORES += ["a%d_%d" % (s, p) for s in range(K) for p in range(NP)]
 SEMAPHORES += ["u%d" % c for c in range(NB)]
@@ -112,6 +111,17 @@ def _far_masks(T, topo, relay, r, p):
     return {far[0]: _pick(stay, 0, half), far[1]: _pick(stay, half, half)}
 
 
+def _id_makers(relay, q):
+    return sorted(r for (r, c) in relay if c == q)
+
+
+def _make_identity(g, T):
+    g.vector.memset(T.one[:, :], 1.0).then_inc(T.sem.fone, 1)
+    g.wait_ge(T.sem.fone, 1)
+    g.affine_select(T.idn[:, :], T.one[:, :], [[-1, B]], AluOpType.is_equal, 0.0, 0, 1).then_inc(T.sem.idg, 1)
+    g.wait_ge(T.sem.idg, 1)
+
+
 def _waiter(queue, T):
     seen = {}
 
@@ -126,7 +136,12 @@ def _relay_program(g, core, T, topo, relay, r, q):
     dst = T.cores[q]
     rid, pid, _ = topo.addr(dst)
     mask = topo.mask(core, dst)
-    sent = 0
+    makers = _id_makers(relay, q)
+    wid = B // len(makers)
+    lo = makers.index(r) * wid
+    _make_identity(g, T)
+    g.remote_dma(T.idn[:, lo:lo + wid], T.idn[:, lo:lo + wid], T.sem.id2, T.sem.snt, pid, rid, mask)
+    sent = _count(mask)
     for p in range(NP):
         lo, hi = _piece_cols(r, p)
         g.wait_ge(T.sem["a0_%d" % p], _count(_far_masks(T, topo, relay, r, p)[q]))
@@ -146,8 +161,12 @@ def _home_program(g, core, T, topo, q, relay):
     def vname(i, c, j):
         return "v%d_%d" % (c * nr + i, j)
 
-    g.vector.memset(T.z[:, 0:1], 1.0).then_inc(T.sem.fill, 1)
-    g.vector.memset(T.z[:, 1:B + 1], 0.0).then_inc(T.sem.fill, 1)
+    makers = _id_makers(relay, q)
+    if makers:
+        id_dep = ("id2", sum(_count(topo.mask(relay[(r, q)], core)) for r in makers))
+    else:
+        _make_identity(g, T)
+        id_dep = ("idg", 1)
     g.vector.memset(T.zer[:, :], 0.0).then_inc(T.sem.fill, 1)
     ldn = [0] * NP
     if q:
@@ -157,15 +176,11 @@ def _home_program(g, core, T, topo, q, relay):
     ldn[0] += 16
     g.sync.dma_start(out=T.in0[:, 2 * B:3 * B], in_=T.wh[:, :]).then_inc(T.sem.ld1, 16)
     ldn[1] += 16
-    wsc("fill", 3)
-    g.scalar.dma_start(out=T.di[:, :], in_=T.z[:, :]).then_inc(T.sem.id1, 16)
     for p in range(1, NP):
         qu = g.scalar if p % 2 else g.sync
         qu.dma_start(out=T.in0[:, (2 + PIECES[p - 1]) * B:(2 + PIECES[p]) * B],
                      in_=T.x[:, PIECES[p - 1] * B:PIECES[p] * B]).then_inc(T.sem["ld%d" % p], 16)
         ldn[p] += 16
-    wsc("id1", 16)
-    g.scalar.dma_start(out=T.idn[:, :], in_=T.di[0:B, :]).then_inc(T.sem.id2, 16)
 
     sent = [0]
     near = [c for c in _consumers(q) if (q, c) not in relay]
@@ -177,12 +192,17 @@ def _home_program(g, core, T, topo, q, relay):
         lo, hi = _piece_cols(q, p)
         wg("ld%d" % p, ldn[p])
         trs = []
-        for c, m in masks.items():
+        for c in sorted(masks, reverse=True):
+            m = masks[c]
             rid, pid, _ = topo.addr(relay[(q, c)])
             trs.append(RemoteDMATransfer(dst_ids=[DstId(rid=rid, pnc=pid)], dma_engine_mask=m,
                                          remote_sem=T.sem["a0_%d" % p], src=T.in0[:, lo:hi], dst=T.in0[:, lo:hi]))
             sent[0] += _count(m)
-        g.remote_dma_fused(trs, local_sem=T.sem.snt)
+        if p == 0:
+            for tr in trs:
+                g.remote_dma_fused([tr], local_sem=T.sem.snt)
+        else:
+            g.remote_dma_fused(trs, local_sem=T.sem.snt)
 
     def send_near(p):
         lo, hi = _piece_cols(q, p)
@@ -211,7 +231,7 @@ def _home_program(g, core, T, topo, q, relay):
     for p in range(1, NP):
         send_far(p)
         send_near(p - 1)
-        if early and hleft and p > 1:
+        if early and hleft and p == 1:
             send_h(hleft.pop(0))
     send_near(NP - 1)
     for k in hleft:
@@ -237,14 +257,19 @@ def _home_program(g, core, T, topo, q, relay):
     for d in range(nr + NB - 1):
         for i in range(min(nr - 1, d), max(0, d - NB + 1) - 1, -1):
             order.append((i, d - i))
-    ops = [("x", 0)]
+    late_up = q - K > 0
+    ahead = min(INFL, len(order)) if late_up else 1
+    ops = [("x", t) for t in range(ahead)]
     for t, (i, c) in enumerate(order):
+        nxt = [("x", t + 1)] if ahead <= t + 1 < len(order) else []
         if c > 0:
             ops.append(("h", t))
+        if i == 0 and late_up:
+            ops += nxt
+            nxt = []
         if i > 0 or a > 0:
             ops.append(("v", t))
-        if t + 1 < len(order):
-            ops.append(("x", t + 1))
+        ops += nxt
     last = {}
     for k, (_, t) in enumerate(ops):
         last[t] = k
@@ -259,7 +284,7 @@ def _home_program(g, core, T, topo, q, relay):
             o = j * W
             if kind == "x":
                 wt(*in_dep(i, _piece_of(c)))
-                wt("id2", 16)
+                wt(*id_dep)
                 if t >= INFL:
                     i0, c0 = order[t - INFL]
                     wt(vname(i0, c0, j), 1)
@@ -281,7 +306,7 @@ def _home_program(g, core, T, topo, q, relay):
             if last[t] == k:
                 ins.then_inc(T.sem["m%d" % bank], 1)
 
-    wv_("fill", 3)
+    wv_("fill", 1)
     for t, (i, c) in enumerate(order):
         s = q - (a + i)
         for j in range(NH):

from concourse.bass import DstId, RemoteDMATransfer
from concourse.mybir import AluOpType

N, NB, B = 9, 8, 128
K = 4
PIECES = (1, 4, 8)
NBANK = 8
NP = len(PIECES)
NH = 2
W = B // NH
INFL = NBANK // NH

SCRATCH = {
    "up": ("sbuf", [128, NB * B], "bfloat16"),
    "idn": ("sbuf", [128, B], "bfloat16"),
    "zer": ("sbuf", [128, B], "bfloat16"),
    "one": ("sbuf", [128, B], "bfloat16"),
}
for _s in range(K):
    SCRATCH["in%d" % _s] = ("sbuf", [128, (NB + 2) * B], "bfloat16")
    SCRATCH["h%d" % _s] = ("sbuf", [128, NB * B], "bfloat16")
for _b in range(NBANK):
    SCRATCH["ps%d" % _b] = ("psum", [128, 512], "float32")

SEMAPHORES = ["fill", "fone", "idg", "id2", "snt", "sty", "stc"]
SEMAPHORES += ["ld%d" % p for p in range(NP)]
SEMAPHORES += ["a%d_%d" % (s, p) for s in range(K) for p in range(NP)]
SEMAPHORES += ["u%d" % c for c in range(NB)]
SEMAPHORES += ["m%d" % b for b in range(NBANK)]
SEMAPHORES += ["v%d_%d" % (n, j) for n in range(K * NB) for j in range(NH)]


def _bits(mask):
    return [e for e in range(32) if (mask >> e) & 1]


def _pick(mask, start, n):
    m = 0
    for e in _bits(mask)[start:start + n]:
        m |= 1 << e
    return m


def _count(mask):
    return len(_bits(mask))


def _xcol(c):
    return B if c == 0 else (c + 2) * B


def _piece_end(p):
    return 2 * B if p == 0 else (2 + PIECES[p]) * B


def _piece_cols(r, p):
    lo = _piece_end(p - 1) if p else (0 if r else B)
    return lo, _piece_end(p)


def _piece_of(c):
    for p in range(NP):
        if c < PIECES[p]:
            return p


def _consumers(r):
    return [q for q in range(r + 1, min(N - 1, r + K - 1) + 1)]


def _hgroups(r):
    if r == 0:
        return [((PIECES[p - 1] if p else 0), PIECES[p]) for p in range(NP)]
    return [(c, c + 1) for c in range(NB)]


def _plan(T, topo):
    cores = list(T.cores)
    relay = {}
    for r in range(N):
        home = cores[r]
        far = [q for q in _consumers(r) if not topo.may_write(home, cores[q])]
        cand = [c for c in range(topo.CORES_PER_CHIP * topo.CHIPS)
                if topo.chip(c) == topo.chip(home) and c not in cores
                and all(topo.may_write(c, cores[q]) for q in far)]
        cand.sort(key=lambda c: (topo.die(c) == topo.die(home), c))
        for j, q in enumerate(far):
            relay[(r, q)] = cand[j]
    return relay


def _far_masks(T, topo, relay, r, p):
    cores = list(T.cores)
    home = cores[r]
    far = [q for q in _consumers(r) if (r, q) in relay]
    near = [q for q in _consumers(r) if (r, q) not in relay]
    if not far:
        return {}
    full = topo.mask(home, relay[(r, far[0])])
    leave = full & topo.mask(home, cores[far[0]])
    stay = full & ~leave
    streams_off = len(near) + (1 if r == 0 and r + K < N else 0)
    wide = NP if streams_off == 0 else (2 if streams_off == 1 else 1)
    if p < wide:
        if len(far) == 1:
            return {far[0]: full}
        return {far[0]: leave, far[1]: stay}
    if len(far) == 1:
        return {far[0]: stay}
    half = _count(stay) // 2
    return {far[0]: _pick(stay, 0, half), far[1]: _pick(stay, half, half)}


def _id_makers(relay, q):
    return sorted(r for (r, c) in relay if c == q)


def _make_identity(g, T):
    g.vector.memset(T.one[:, :], 1.0).then_inc(T.sem.fone, 1)
    g.wait_ge(T.sem.fone, 1)
    g.affine_select(T.idn[:, :], T.one[:, :], [[-1, B]], AluOpType.is_equal, 0.0, 0, 1).then_inc(T.sem.idg, 1)
    g.wait_ge(T.sem.idg, 1)


def _waiter(queue, T):
    seen = {}

    def w(name, val):
        if seen.get(name, 0) < val:
            queue.wait_ge(T.sem[name], val)
            seen[name] = val
    return w


def _relay_program(g, core, T, topo, relay, r, q):
    dst = T.cores[q]
    rid, pid, _ = topo.addr(dst)
    mask = topo.mask(core, dst)
    makers = _id_makers(relay, q)
    wid = B // len(makers)
    lo = makers.index(r) * wid
    _make_identity(g, T)
    g.remote_dma(T.idn[:, lo:lo + wid], T.idn[:, lo:lo + wid], T.sem.id2, T.sem.snt, pid, rid, mask)
    sent = _count(mask)
    for p in range(NP):
        lo, hi = _piece_cols(r, p)
        g.wait_ge(T.sem["a0_%d" % p], _count(_far_masks(T, topo, relay, r, p)[q]))
        g.remote_dma(T["in%d" % (q - r)][:, lo:hi], T.in0[:, lo:hi], T.sem["a%d_%d" % (q - r, p)], T.sem.snt,
                     pid, rid, mask)
        sent += _count(mask)
    g.wait_ge(T.sem.snt, sent)


def _home_program(g, core, T, topo, q, relay):
    cores = list(T.cores)
    a = max(0, q - K + 1)
    nr = q - a + 1
    wt, wv_, wg = _waiter(g.tensor, T), _waiter(g.vector, T), _waiter(g, T)
    wsy, wsc = _waiter(g.sync, T), _waiter(g.scalar, T)

    def vname(i, c, j):
        return "v%d_%d" % (c * nr + i, j)

    makers = _id_makers(relay, q)
    if makers:
        id_dep = ("id2", sum(_count(topo.mask(relay[(r, q)], core)) for r in makers))
    else:
        _make_identity(g, T)
        id_dep = ("idg", 1)
    g.vector.memset(T.zer[:, :], 0.0).then_inc(T.sem.fill, 1)
    ldn = [0] * NP
    if q:
        g.sync.dma_start(out=T.in0[:, 0:B], in_=T.wv[:, :]).then_inc(T.sem.ld0, 16)
        ldn[0] += 16
    g.scalar.dma_start(out=T.in0[:, B:2 * B], in_=T.x[:, 0:B]).then_inc(T.sem.ld0, 16)
    ldn[0] += 16
    g.sync.dma_start(out=T.in0[:, 2 * B:3 * B], in_=T.wh[:, :]).then_inc(T.sem.ld1, 16)
    ldn[1] += 16
    for p in range(1, NP):
        qu = g.scalar if p % 2 else g.sync
        qu.dma_start(out=T.in0[:, (2 + PIECES[p - 1]) * B:(2 + PIECES[p]) * B],
                     in_=T.x[:, PIECES[p - 1] * B:PIECES[p] * B]).then_inc(T.sem["ld%d" % p], 16)
        ldn[p] += 16

    sent = [0]
    near = [c for c in _consumers(q) if (q, c) not in relay]

    def send_far(p):
        masks = _far_masks(T, topo, relay, q, p)
        if not masks:
            return
        lo, hi = _piece_cols(q, p)
        wg("ld%d" % p, ldn[p])
        trs = []
        for c in sorted(masks, reverse=True):
            m = masks[c]
            rid, pid, _ = topo.addr(relay[(q, c)])
            trs.append(RemoteDMATransfer(dst_ids=[DstId(rid=rid, pnc=pid)], dma_engine_mask=m,
                                         remote_sem=T.sem["a0_%d" % p], src=T.in0[:, lo:hi], dst=T.in0[:, lo:hi]))
            sent[0] += _count(m)
        if p == 0:
            for tr in trs:
                g.remote_dma_fused([tr], local_sem=T.sem.snt)
        else:
            g.remote_dma_fused(trs, local_sem=T.sem.snt)

    def send_near(p):
        lo, hi = _piece_cols(q, p)
        for c in near:
            wg("ld%d" % p, ldn[p])
            rid, pid, _ = topo.addr(cores[c])
            m = topo.mask(core, cores[c])
            g.remote_dma(T["in%d" % (c - q)][:, lo:hi], T.in0[:, lo:hi], T.sem["a%d_%d" % (c - q, p)], T.sem.snt,
                         pid, rid, m)
            sent[0] += _count(m)

    def send_h(k):
        c0, c1 = _hgroups(q)[k]
        dst = cores[q + K]
        rid, pid, _ = topo.addr(dst)
        m = topo.mask(core, dst)
        for c in range(c0, c1):
            for j in range(NH):
                wg(vname(nr - 1, c, j), 1)
        g.remote_dma(T.up[:, c0 * B:c1 * B], T.h0[:, c0 * B:c1 * B], T.sem["u%d" % k], T.sem.snt, pid, rid, m)
        sent[0] += _count(m)

    hleft = list(range(len(_hgroups(q)))) if q + K < N else []
    early = q == 0
    send_far(0)
    for p in range(1, NP):
        send_far(p)
        send_near(p - 1)
        if early and hleft and p == 1:
            send_h(hleft.pop(0))
    send_near(NP - 1)
    for k in hleft:
        send_h(k)
    if sent[0]:
        g.wait_ge(T.sem.snt, sent[0])

    def in_dep(i, p):
        r = a + i
        if r == q:
            return "ld%d" % p, ldn[p]
        src = relay.get((r, q), cores[r])
        return "a%d_%d" % (q - r, p), _count(topo.mask(src, core))

    up_n = _count(topo.mask(cores[q - K], core)) if a else 0
    up_k = {}
    if a:
        for k, (c0, c1) in enumerate(_hgroups(q - K)):
            for c in range(c0, c1):
                up_k[c] = k

    order = []
    for d in range(nr + NB - 1):
        for i in range(min(nr - 1, d), max(0, d - NB + 1) - 1, -1):
            order.append((i, d - i))
    late_up = q - K > 0
    ahead = min(INFL, len(order)) if late_up else 1
    ops = [("x", t) for t in range(ahead)]
    for t, (i, c) in enumerate(order):
        nxt = [("x", t + 1)] if ahead <= t + 1 < len(order) else []
        if c > 0:
            ops.append(("h", t))
        if i == 0 and late_up:
            ops += nxt
            nxt = []
        if i > 0 or a > 0:
            ops.append(("v", t))
        ops += nxt
    last = {}
    for k, (_, t) in enumerate(ops):
        last[t] = k

    for k, (kind, t) in enumerate(ops):
        i, c = order[t]
        s = q - (a + i)
        inb = T["in%d" % s]
        for j in range(NH):
            bank = (t * NH + j) % NBANK
            out = T["ps%d" % bank][:, 0:W]
            o = j * W
            if kind == "x":
                wt(*in_dep(i, _piece_of(c)))
                wt(*id_dep)
                if t >= INFL:
                    i0, c0 = order[t - INFL]
                    wt(vname(i0, c0, j), 1)
                ins = g.tensor.matmul(out, T.idn[:, :], inb[:, _xcol(c) + o:_xcol(c) + o + W], True, last[t] == k)
            elif kind == "h":
                wt(*in_dep(i, 1))
                wt(vname(i, c - 1, j), 1)
                ins = g.tensor.matmul(out, inb[:, 2 * B:3 * B], T["h%d" % s][:, (c - 1) * B + o:(c - 1) * B + o + W],
                                      False, last[t] == k)
            else:
                wt(*in_dep(i, 0))
                if i:
                    wt(vname(i - 1, c, j), 1)
                    rhs = T["h%d" % (s + 1)][:, c * B + o:c * B + o + W]
                else:
                    wt("u%d" % up_k[c], up_n)
                    rhs = T.up[:, c * B + o:c * B + o + W]
                ins = g.tensor.matmul(out, inb[:, 0:B], rhs, False, last[t] == k)
            if last[t] == k:
                ins.then_inc(T.sem["m%d" % bank], 1)

    wv_("fill", 1)
    for t, (i, c) in enumerate(order):
        s = q - (a + i)
        for j in range(NH):
            u = t * NH + j
            wv_("m%d" % (u % NBANK), u // NBANK + 1)
            g.vector.tensor_tensor(T["h%d" % s][:, c * B + j * W:c * B + (j + 1) * W],
                                   T["ps%d" % (u % NBANK)][:, 0:W], T.zer[:, 0:W],
                                   AluOpType.max).then_inc(T.sem[vname(i, c, j)], 1)

    groups = [(0, 4), (4, 8)] if q + K < N else [(0, 4), (4, 6), (6, 7), (7, 8)]
    tot = {"sty": 0, "stc": 0}
    for k, (c0, c1) in enumerate(groups):
        qu, w, name = ((g.sync, wsy, "sty"), (g.scalar, wsc, "stc"))[k % 2]
        for c in range(c0, c1):
            for j in range(NH):
                w(vname(nr - 1, c, j), 1)
        qu.dma_start(out=T.y[:, c0 * B:c1 * B], in_=T.h0[:, c0 * B:c1 * B]).then_inc(T.sem[name], 16)
        tot[name] += 16
    wsy("sty", tot["sty"])
    wsc("stc", tot["stc"])


def rank_program(g, core, T, topo):
    relay = _plan(T, topo)
    q = T.rank_of(core)
    if q is not None:
        _home_program(g, core, T, topo, q, relay)
        return
    for (r, c), hc in relay.items():
        if hc == core:
            _relay_program(g, core, T, topo, relay, r, c)
            return
